import numpy as np
import ml_dtypes


def mxq(x, axis, fmt="e4m3"):
    dtype, down = {"e4m3": (ml_dtypes.float8_e4m3fn, 7), "e5m2": (ml_dtypes.float8_e5m2, 14)}[fmt]
    v = np.moveaxis(np.asarray(x, np.float32).astype(ml_dtypes.bfloat16).astype(np.float64), axis, -1)
    blocks = v.reshape(v.shape[:-1] + (-1, 32))
    amax = np.abs(blocks).max(-1, keepdims=True)
    byte = np.maximum(np.where(amax > 0, np.frexp(amax)[1] - 1 + 127, 0) - down, 1)
    scale = np.exp2(byte - 127.0)
    codes = (blocks / scale).astype(np.float32).astype(dtype).astype(np.float64)
    return np.moveaxis((codes * scale).reshape(v.shape), -1, axis)


WIDE = False


def mx_kscale(k):
    if not WIDE:
        return np.ones(k)
    levels = np.array([10, -10, 5, -5, 0])
    if k % 512:
        return np.exp2(np.random.permutation(np.resize(levels, k // 32))).repeat(32)
    a = np.empty((k // 512, 16))
    for p in range(k // 512):
        a[p, :8] = np.random.permutation(np.resize(levels, 8))
        for g in range(8):
            far = levels[np.abs(levels - a[p, g]) >= 10]
            a[p, g + 8] = far[np.random.randint(len(far))]
    return np.exp2(a.ravel()).repeat(32)


def f64(x):
    return np.asarray(x).astype(np.float64)


def striped(idx):
    return np.tile(idx.reshape(-1, 16).T, (8, 1)).astype(np.uint16)


def unstriped(offs):
    return offs[:16].T.reshape(-1).astype(np.int64)


E2M1 = np.array([0.0, 0.5, 1.0, 1.5, 2.0, 3.0, 4.0, 6.0, -0.0, -0.5, -1.0, -1.5, -2.0, -3.0, -4.0, -6.0])


def pack_weight(w, fmt):
    k, n = w.shape
    w = f64(np.asarray(w, np.float32).astype(ml_dtypes.bfloat16)).reshape(k // 32, 32, n)
    amax = np.abs(w).max(1)
    if fmt == "e4m3":
        byte = np.frexp(amax)[1] - 1 + 127 - 7
    else:
        mant, ex = np.frexp(amax / 6.0)
        byte = np.where(mant > 0.5, ex, ex - 1) + 127
    byte = np.clip(np.where(amax > 0, byte, 1), 1, 254)
    scaled = (w * np.exp2(127.0 - byte)[:, None, :]).reshape(k, n).astype(np.float32)
    by_word = np.ascontiguousarray(scaled.reshape(k // 512, 128, 4, n).transpose(0, 1, 3, 2))
    if fmt == "e4m3":
        words = by_word.astype(ml_dtypes.float8_e4m3fn).view(np.uint8)
    else:
        c = by_word.astype(ml_dtypes.float4_e2m1fn).view(np.uint8) & 0xF
        words = (c[..., 0::2] | (c[..., 1::2] << 4)).reshape(k // 512, 128, 2 * n)
    return np.ascontiguousarray(words), np.ascontiguousarray(byte.astype(np.uint8).reshape(k // 512, 16, n))


def unpack_weight(words, scales, fmt):
    g, _, n = scales.shape
    words = np.ascontiguousarray(words).reshape(g, 128, n, -1)
    if fmt == "e4m3":
        vals = words.view(ml_dtypes.float8_e4m3fn).astype(np.float64)
    else:
        nib = np.empty((g, 128, n, 4), np.uint8)
        nib[..., 0::2] = words & 0xF
        nib[..., 1::2] = words >> 4
        vals = E2M1[nib]
    vals = vals * np.repeat(np.exp2(scales.astype(np.float64) - 127.0), 8, axis=1)[..., None]
    return vals.transpose(0, 1, 3, 2).reshape(g * 512, n)


def gelu(v):
    return 0.5 * v * (1.0 + np.tanh(np.sqrt(2.0 / np.pi) * (v + 0.044715 * v**3)))


K, H, T, S, T2, P = 1536, 1024, 2048, 512, 1024, 512

def setup_inputs():
    n = np.random.standard_normal
    s = mx_kscale(K)[:, None]
    u = mx_kscale(H)[:, None]
    d = {}
    d["tab_words"], d["tab_scales"] = pack_weight(n((K, T)) * s, "e4m3")
    d["offs"] = striped(np.random.permutation(T)[:S])
    d["offs2"] = striped(np.random.permutation(T2)[:S])
    d["offs3"] = striped(np.random.permutation(T2)[:P])
    d["w1"] = (1.5 * n((K, H)) / K**0.5 / s).astype(np.float32)
    d["b1"] = (0.6 * n(H)).astype(np.float32)
    d["ga"] = (np.exp(0.3 * n(H)) * u[:, 0]).astype(np.float32)
    d["w4_words"], d["w4_scales"] = pack_weight(0.8 * n((K, H)) / K**0.5 / s * u.T, "e2m1")
    d["wgs"] = np.exp(0.3 * n((128, S))).astype(np.float32)
    d["page0"] = (n((H, T2)) * u).astype(np.float32)
    d["wa"] = (0.7 * np.exp(0.3 * n(H))).astype(np.float32)
    d["gx"] = (n(H) / H**0.5 / u[:, 0]**2).astype(np.float32)
    d["slot"] = np.exp(0.3 * n(T2)).astype(np.float32)
    d["base"] = (0.8 * n((T2, P))).astype(np.float32)
    return d

def reference(tab_words, tab_scales, offs, offs2, offs3, w1, b1, ga, w4_words, w4_scales, wgs, page0, wa, gx, slot, base):
    v = unpack_weight(tab_words, tab_scales, "e4m3")[:, unstriped(offs)]
    w4 = unpack_weight(w4_words, w4_scales, "e2m1")
    t1 = (mxq(f64(w1), 0, "e4m3").T @ v) + f64(b1)[:, None]
    f = t1 / (1.0 + np.exp(-t1))
    h = f * f64(ga)[:, None] + (w4.T @ v)
    page = f64(page0).copy()
    page[:, unstriped(offs2)] = np.tile(f64(wgs), (H // 128, 1)) * h
    x = page[:, unstriped(offs3)]
    x = (x - np.abs(x) * f64(wa)[:, None]) * f64(gx)[:, None]
    e = mxq(page, 0, "e4m3").T @ mxq(x, 0, "e4m3")
    return e * f64(slot)[:, None] + f64(base)

@@ -1,0 +1,368 @@
+from contextlib import ExitStack
+
+import concourse.mybir as mybir
+
+K, H, T, S, T2, NX = 1536, 1024, 2048, 512, 1024, 512
+FLOPS = 2 * (2 * K * H * S + H * T2 * NX)
+
+F32 = mybir.dt.float32
+BF16 = mybir.dt.bfloat16
+I32 = mybir.dt.int32
+U32 = mybir.dt.uint32
+U16 = mybir.dt.uint16
+U8 = mybir.dt.uint8
+FP8X4 = mybir.dt.float8_e4m3fn_x4
+FP4X4 = mybir.dt.float4_e2m1fn_x4
+ALU = mybir.AluOpType
+ACT = mybir.ActivationFunctionType
+
+P = 128
+PACK = 4
+KP = P * PACK
+NA = K // KP
+NB = H // KP
+NT = NB * PACK
+NM = T2 // P
+CH = 256
+NC = T2 // CH
+SPLIT = 80
+
+
+def tile_list_arousal_exemplar_scores_kernel(
+    tc, tab_words, tab_scales, offs, offs2, offs3, w1, b1, ga, w4_words, w4_scales, wgs, page0, wa, gx, slot, base, out
+):
+    nc = tc.nc
+    with ExitStack() as ctx:
+        keep = ctx.enter_context(tc.tile_pool(name="keep", bufs=1))
+        psum = ctx.enter_context(tc.psum_pool(name="psum", bufs=1))
+
+        def sb(shape, dtype, name, tag=None, bufs=1):
+            return keep.tile(shape, dtype, name=name, tag=tag or name, bufs=bufs, align_bytes=64)
+
+        def bank(k, name):
+            return psum.tile([P, S], F32, name=name, tag="bank%d" % k)
+
+        o1 = keep.tile([P, S // 16], U16, name="o1")
+        o2 = keep.tile([P, S // 16], U16, name="o2")
+        o3 = keep.tile([P, NX // 16], U16, name="o3")
+
+        tsc = sb([P, NA * T], U8, "tsc")
+        w4s_raw = sb([P, NA * H], U8, "w4s_raw")
+        nc.vector.memset(tsc[:].bitcast(I32), 0)
+        nc.gpsimd.memset(w4s_raw[:].bitcast(I32), 0)
+
+        def load_scales(eng, plane, dram):
+            rows = dram.bitcast(I32).rearrange("a (q r) n -> r q a n", r=4)
+            for r in range(4):
+                eng.dma_start(out=plane[r:P:32, :].bitcast(I32).rearrange("q (a n) -> q a n", a=NA), in_=rows[r])
+
+        tabw = [sb([P, T], I32, "tabw%d" % a) for a in range(NA)]
+        w1raw = {}
+
+        def load_tab(a):
+            nc.sync.dma_start(out=tabw[a][:], in_=tab_words[a].rearrange("p n t -> p (n t)").bitcast(I32))
+
+        def load_w1(a, b):
+            w1raw[a, b] = sb([P, PACK, KP], F32, "w1raw%d%d" % (a, b), tag="big", bufs=4)
+            rows = w1[a * KP : (a + 1) * KP, b * KP : (b + 1) * KP]
+            nc.sync.dma_start(out=w1raw[a, b][:], in_=rows.rearrange("(p j) c -> p j c", j=PACK))
+
+        def load_vec(dram, name):
+            t = sb([P, NB, PACK], F32, name)
+            nc.sync.dma_start(out=t[:], in_=dram.rearrange("(b p i) -> p b i", b=NB, i=PACK))
+            return t
+
+        page = [sb([P, T2], F32, "page%d" % n) for n in range(NT)]
+        page_rows = page0.rearrange("(b p i) m -> b i p m", b=NB, i=PACK)
+
+        def load_page(n):
+            nc.sync.dma_start(out=page[n][:], in_=page_rows[n // PACK, n % PACK])
+
+        wgs_rows = wgs.rearrange("(q i) j -> q i j", i=PACK)
+        wg_first = sb([P, S], F32, "wg_first")
+        wg_rest = sb([P, PACK - 1, S], F32, "wg_rest")
+
+        nc.sync.dma_start(o1[:], offs)
+        load_tab(0)
+        load_w1(0, 0)
+        load_scales(nc.sync, tsc, tab_scales)
+        load_tab(1)
+        load_scales(nc.sync, w4s_raw, w4_scales)
+        b1t = load_vec(b1, "b1t")
+        load_w1(1, 0)
+        gat = load_vec(ga, "gat")
+        w4_raw = sb([P, NA, 2 * H], U8, "w4_raw")
+        nc.sync.dma_start(out=w4_raw[:].bitcast(I32), in_=w4_words.bitcast(I32).rearrange("a p n -> p a n"))
+        load_tab(2)
+        nc.sync.dma_start(o2[:], offs2)
+        load_w1(2, 0)
+        for q in range(4):
+            nc.sync.dma_start(out=wg_first[32 * q : 32 * q + 32, :], in_=wgs_rows[:, 0, :])
+        load_page(0)
+        nc.sync.dma_start(o3[:], offs3)
+        load_page(1)
+        for q in range(4):
+            nc.sync.dma_start(out=wg_rest[32 * q : 32 * q + 32, :, :], in_=wgs_rows[:, 1:PACK, :])
+        load_w1(0, 1)
+        load_w1(1, 1)
+        load_w1(2, 1)
+        load_page(2)
+        wat = load_vec(wa, "wat")
+        gxt = load_vec(gx, "gxt")
+        for n in range(3, NT):
+            load_page(n)
+
+        vq = [sb([P, S], U32, "vq%d" % a) for a in range(NA)]
+        vs = [sb([P, S], U8, "vs%d" % a) for a in range(NA)]
+        w1q_0 = sb([P, NA * KP], U32, "w1q_0")
+        w1q_1 = sb([P, (NA - 1) * KP], U32, "w1q_1", tag="stage")
+        w1q_2 = sb([P, KP], U32, "w1q_2", tag="w1q_b1")
+        w1q = {(a, 0): w1q_0[:, a * KP : (a + 1) * KP] for a in range(NA)}
+        w1q.update({(a, 1): w1q_1[:, a * KP : (a + 1) * KP] for a in range(NA - 1)})
+        w1q[NA - 1, 1] = w1q_2[:]
+        w1s = {}
+
+        def gather_tab(a):
+            nc.vector.tensor_copy(out=vs[a][:], in_=tsc[:, a * T : (a + 1) * T].indirect(o1[:]))
+            nc.vector.tensor_copy(out=vq[a][:], in_=tabw[a][:].bitcast(U32).indirect(o1[:]))
+
+        def cast_w1(a, b, split):
+            if (a, b) == (NA - 1, NB - 1):
+                wbf = sb([P, PACK * KP], BF16, "wbf%d%d" % (a, b), tag="hold")
+            else:
+                wbf = sb([P, PACK * KP], BF16, "wbf%d%d" % (a, b), tag="wbf", bufs=2)
+            dst = wbf[:].rearrange("p (t m j) -> p m j t", t=PACK, j=PACK)
+            srcv = w1raw[a, b][:].rearrange("p j (m t) -> p m j t", t=PACK)
+            if split:
+                nc.vector.tensor_copy(out=dst[:, :SPLIT], in_=srcv[:, :SPLIT])
+                nc.scalar.copy(out=dst[:, SPLIT:], in_=srcv[:, SPLIT:])
+            else:
+                nc.scalar.copy(out=dst, in_=srcv)
+            return wbf
+
+        def quant_w1(a, b, wbf, pieces):
+            w1s[a, b] = sb([P, KP], U8, "w1s%d%d" % (a, b))
+            for c0, c1 in pieces:
+                nc.vector.quantize_mx(
+                    out=w1q[a, b][:, c0:c1].bitcast(FP8X4),
+                    scales=w1s[a, b][:, c0:c1],
+                    in_=wbf[:, PACK * c0 : PACK * c1],
+                )
+
+        w4q = sb([P, NA * 2 * H], U8, "w4q")
+        w4s = sb([P, NA * H], U8, "w4s")
+        cneg = sb([P, NB, PACK], F32, "cneg")
+
+        wb = cast_w1(0, 0, False)
+        gather_tab(0)
+        quant_w1(0, 0, wb, [(0, KP)])
+        nc.vector.tensor_copy(
+            out=w4s[:].rearrange("p (g t m) -> p g m t", t=PACK, m=P),
+            in_=w4s_raw[:].rearrange("p (g m t) -> p g m t", t=PACK, m=P),
+        )
+        wb = cast_w1(1, 0, False)
+        gather_tab(1)
+        quant_w1(1, 0, wb, [(0, KP)])
+        nc.vector.tensor_copy(
+            out=w4q[:].bitcast(U16).rearrange("p (g t m) -> p g m t", t=PACK, m=P),
+            in_=w4_raw[:].rearrange("p a n -> p (a n)").bitcast(U16).rearrange("p (g m t) -> p g m t", t=PACK, m=P),
+        )
+        gather_tab(2)
+        wb = cast_w1(2, 0, True)
+        quant_w1(2, 0, wb, [(0, P), (P, 2 * P), (2 * P, KP)])
+
+        fs = {}
+        ys = {}
+        hs = {}
+
+        def stage1_t(n):
+            b, i = divmod(n, PACK)
+            t1 = bank(n % 2 if b == 0 else n, "t1_%d" % n)
+            cols = slice(i * P, (i + 1) * P)
+            for a in range(NA):
+                nc.tensor.matmul_mx(
+                    out=t1[:],
+                    lhsT=w1q[a, b][:, cols].bitcast(FP8X4),
+                    lhsT_scale=w1s[a, b][:, cols],
+                    rhs=vq[a][:].bitcast(FP8X4),
+                    rhs_scale=vs[a][:],
+                    start=(a == 0),
+                    stop=(a == NA - 1),
+                )
+            fs[n] = sb([P, S], F32, "f%d" % n, tag="f", bufs=NT)
+            nc.scalar.activation(out=fs[n][:], in_=t1[:], func=ACT.Silu, bias=b1t[:, b, i : i + 1])
+
+        def stage1_y(n):
+            b, i = divmod(n, PACK)
+            y4 = bank(2 + n % 2, "y4_%d" % n)
+            for a in range(NA):
+                c0 = a * H + b * KP + i * P
+                nc.tensor.matmul_mx(
+                    out=y4[:],
+                    lhsT=w4q[:, 2 * c0 : 2 * (c0 + P)].bitcast(FP4X4),
+                    lhsT_scale=w4s[:, c0 : c0 + P],
+                    rhs=vq[a][:].bitcast(FP8X4),
+                    rhs_scale=vs[a][:],
+                    start=(a == 0),
+                    stop=(a == NA - 1),
+                )
+            ys[n] = y4
+
+        def combine(n):
+            b, i = divmod(n, PACK)
+            if n == PACK - 2:
+                hs[n] = sb([P, S], F32, "h%d" % n, tag="hold")
+            else:
+                hs[n] = sb([P, S], F32, "h%d" % n, tag="h", bufs=3)
+            nc.vector.scalar_tensor_tensor(
+                out=hs[n][:], in0=fs[n][:], scalar=gat[:, b, i : i + 1], in1=ys[n][:], op0=ALU.mult, op1=ALU.add
+            )
+
+        def scatter(n):
+            i = n % PACK
+            wg = wg_first[:] if i == 0 else wg_rest[:, i - 1, :]
+            nc.vector.tensor_tensor(out=page[n][:].indirect(o2[:]), in0=hs[n][:], in1=wg, op=ALU.mult)
+
+        g4 = [sb([P, PACK, NX], F32, "g4_%d" % b) for b in range(NB)]
+        m4 = {}
+        stage = {}
+
+        def pick(n):
+            b, i = divmod(n, PACK)
+            nc.vector.tensor_copy(out=g4[b][:, i, :], in_=page[n][:].indirect(o3[:]))
+
+        def slope(n):
+            b, i = divmod(n, PACK)
+            sg = sb([P, NX], F32, "sg%d" % n, tag="w1q_b1")
+            nc.scalar.activation(out=sg[:], in_=g4[b][:, i, :], func=ACT.Sign, scale=-1.0)
+            nc.scalar.activation(
+                out=m4[b][:, i, :],
+                in_=sg[:],
+                func=ACT.Identity,
+                scale=cneg[:, b, i : i + 1],
+                bias=gxt[:, b, i : i + 1],
+            )
+
+        pbf = {}
+        pq = {}
+        ps = {}
+
+        def round_page(n):
+            b, i = divmod(n, PACK)
+            if i == 0:
+                stage[b] = sb([P, PACK - 1, T2], BF16, "stage%d" % b, tag="stage")[:]
+            if i < PACK - 1:
+                nc.scalar.copy(out=stage[b][:, i, :], in_=page[n][:])
+            if i == PACK - 2:
+                for c in range(NC):
+                    pbf[b, c] = sb([P, CH * PACK], BF16, "pbf%d%d" % (b, c), tag="pbf%d%d" % (b, c))
+                    nc.scalar.copy(
+                        out=pbf[b, c][:].rearrange("p (c u t) -> p c t u", u=4, t=PACK)[:, :, : PACK - 1, :],
+                        in_=stage[b][:, :, c * CH : (c + 1) * CH].rearrange("p t (c u) -> p c t u", u=4),
+                    )
+            if i == PACK - 1:
+                for c in range(NC):
+                    nc.scalar.copy(
+                        out=pbf[b, c][:].rearrange("p (c t) -> p c t", t=PACK)[:, :, PACK - 1],
+                        in_=page[n][:, c * CH : (c + 1) * CH],
+                    )
+
+        def quant_page(b, c):
+            pq[b, c] = sb([P, CH], U32, "pq%d%d" % (b, c))
+            ps[b, c] = sb([P, CH], U8, "ps%d%d" % (b, c))
+            nc.vector.quantize_mx(out=pq[b, c][:].bitcast(FP8X4), scales=ps[b, c][:], in_=pbf[b, c][:])
+
+        xbf = {}
+        xq = {}
+        xs = {}
+
+        def make_x(b):
+            xbf[b] = sb([P, NX * PACK], BF16, "xbf%d" % b, tag="wbf", bufs=2)
+            nc.vector.tensor_tensor(
+                out=xbf[b][:].rearrange("p (c u t) -> p c t u", u=4, t=PACK),
+                in0=g4[b][:].rearrange("p t (c u) -> p c t u", u=4),
+                in1=m4[b].rearrange("p t (c u) -> p c t u", u=4),
+                op=ALU.mult,
+            )
+
+        def quant_x(b):
+            xq[b] = sb([P, NX], U32, "xq%d" % b)
+            xs[b] = sb([P, NX], U8, "xs%d" % b)
+            nc.vector.quantize_mx(out=xq[b][:].bitcast(FP8X4), scales=xs[b][:], in_=xbf[b][:])
+
+        es = {}
+
+        def stage2(b, mt):
+            if b == 0:
+                es[mt] = bank(mt, "e%d" % mt)
+            c, r = divmod(mt * P, CH)
+            nc.tensor.matmul_mx(
+                out=es[mt][:],
+                lhsT=pq[b, c][:, r : r + P].bitcast(FP8X4),
+                lhsT_scale=ps[b, c][:, r : r + P],
+                rhs=xq[b][:].bitcast(FP8X4),
+                rhs_scale=xs[b][:],
+                start=(b == 0),
+                stop=(b == NB - 1),
+            )
+
+        for n in range(PACK):
+            stage1_t(n)
+            if n < 2:
+                stage1_y(n)
+        combine(0)
+        stage1_y(2)
+        for n in range(NT):
+            scatter(n)
+            if n == 0:
+                for a in range(NA):
+                    quant_w1(a, 1, cast_w1(a, 1, False), [(0, KP)])
+            if n == 1:
+                for n1 in range(PACK, NT):
+                    stage1_t(n1)
+            if n + 1 < NT:
+                combine(n + 1)
+            if n + 3 < NT:
+                stage1_y(n + 3)
+            pick(n)
+
+        nc.gpsimd.tensor_tensor(out=cneg[:], in0=gxt[:], in1=wat[:], op=ALU.mult)
+        for b in range(NB):
+            m4[b] = sb([P, PACK, NX], F32, "m4_%d" % b, tag=("w1q_0", "w4_raw")[b])[:]
+        for n in range(NT):
+            round_page(n)
+            slope(n)
+        make_x(0)
+        for c in range(NC):
+            quant_page(0, c)
+        quant_x(0)
+
+        base_rows = base.rearrange("(t p) j -> p t j", p=P)
+        baset = []
+        for u in range(2):
+            baset.append(sb([P, PACK, NX], F32, "base%d" % u, tag="big", bufs=4))
+            nc.sync.dma_start(out=baset[u][:], in_=base_rows[:, PACK * u : PACK * (u + 1), :])
+        slott = sb([P, NM], F32, "slott")
+        with nc.allow_non_contiguous_dma(reason="one factor for each output row"):
+            nc.sync.dma_start(out=slott[:], in_=slot.rearrange("(t p) -> p t", p=P))
+
+        for mt in (4, 5, 6, 7, 0, 1, 2, 3):
+            stage2(0, mt)
+        quant_page(1, 0)
+        make_x(1)
+        quant_page(1, 1)
+        quant_x(1)
+        quant_page(1, 2)
+        quant_page(1, 3)
+        for mt in range(NM):
+            stage2(1, mt)
+            res = sb([P, NX], F32, "res%d" % mt, tag="f", bufs=NT)
+            nc.vector.scalar_tensor_tensor(
+                out=res[:],
+                in0=es[mt][:],
+                scalar=slott[:, mt : mt + 1],
+                in1=baset[mt // PACK][:, mt % PACK, :],
+                op0=ALU.mult,
+                op1=ALU.add,
+            )
+            nc.sync.dma_start(out=out[mt * P : (mt + 1) * P, :], in_=res[:])

@@ -49,7 +49,7 @@ def tile_list_arousal_exemplar_scores_kernel(
         tsc = sb([P, NA * T], U8, "tsc")
         w4s_raw = sb([P, NA * H], U8, "w4s_raw")
         nc.vector.memset(tsc[:].bitcast(I32), 0)
-        nc.gpsimd.memset(w4s_raw[:].bitcast(I32), 0)
+        nc.vector.memset(w4s_raw[:].bitcast(I32), 0)
 
         def load_scales(eng, plane, dram):
             rows = dram.bitcast(I32).rearrange("a (q r) n -> r q a n", r=4)
@@ -63,7 +63,10 @@ def tile_list_arousal_exemplar_scores_kernel(
             nc.sync.dma_start(out=tabw[a][:], in_=tab_words[a].rearrange("p n t -> p (n t)").bitcast(I32))
 
         def load_w1(a, b):
-            w1raw[a, b] = sb([P, PACK, KP], F32, "w1raw%d%d" % (a, b), tag="big", bufs=4)
+            if (a, b) == (NA - 1, NB - 1):
+                w1raw[a, b] = sb([P, PACK, KP], F32, "w1raw%d%d" % (a, b), tag="raw_last")
+            else:
+                w1raw[a, b] = sb([P, PACK, KP], F32, "w1raw%d%d" % (a, b), tag="big", bufs=3)
             rows = w1[a * KP : (a + 1) * KP, b * KP : (b + 1) * KP]
             nc.sync.dma_start(out=w1raw[a, b][:], in_=rows.rearrange("(p j) c -> p j c", j=PACK))
 
@@ -85,17 +88,17 @@ def tile_list_arousal_exemplar_scores_kernel(
         nc.sync.dma_start(o1[:], offs)
         load_tab(0)
         load_w1(0, 0)
-        load_scales(nc.sync, tsc, tab_scales)
+        load_scales(nc.gpsimd, tsc, tab_scales)
         load_tab(1)
-        load_scales(nc.sync, w4s_raw, w4_scales)
-        b1t = load_vec(b1, "b1t")
+        load_scales(nc.gpsimd, w4s_raw, w4_scales)
         load_w1(1, 0)
-        gat = load_vec(ga, "gat")
         w4_raw = sb([P, NA, 2 * H], U8, "w4_raw")
         nc.sync.dma_start(out=w4_raw[:].bitcast(I32), in_=w4_words.bitcast(I32).rearrange("a p n -> p a n"))
         load_tab(2)
-        nc.sync.dma_start(o2[:], offs2)
         load_w1(2, 0)
+        b1t = load_vec(b1, "b1t")
+        gat = load_vec(ga, "gat")
+        nc.sync.dma_start(o2[:], offs2)
         for q in range(4):
             nc.sync.dma_start(out=wg_first[32 * q : 32 * q + 32, :], in_=wgs_rows[:, 0, :])
         load_page(0)
@@ -123,16 +126,16 @@ def tile_list_arousal_exemplar_scores_kernel(
         w1s = {}
 
         def gather_tab(a):
-            nc.vector.tensor_copy(out=vs[a][:], in_=tsc[:, a * T : (a + 1) * T].indirect(o1[:]))
             nc.vector.tensor_copy(out=vq[a][:], in_=tabw[a][:].bitcast(U32).indirect(o1[:]))
+            nc.vector.tensor_copy(out=vs[a][:], in_=tsc[:, a * T : (a + 1) * T].indirect(o1[:]))
 
         def cast_w1(a, b, split):
             if (a, b) == (NA - 1, NB - 1):
                 wbf = sb([P, PACK * KP], BF16, "wbf%d%d" % (a, b), tag="hold")
             else:
                 wbf = sb([P, PACK * KP], BF16, "wbf%d%d" % (a, b), tag="wbf", bufs=2)
-            dst = wbf[:].rearrange("p (t m j) -> p m j t", t=PACK, j=PACK)
-            srcv = w1raw[a, b][:].rearrange("p j (m t) -> p m j t", t=PACK)
+            dst = wbf[:].rearrange("p (t m j) -> p m t j", t=PACK, j=PACK)
+            srcv = w1raw[a, b][:].rearrange("p j (m t) -> p m t j", t=PACK)
             if split:
                 nc.vector.tensor_copy(out=dst[:, :SPLIT], in_=srcv[:, :SPLIT])
                 nc.scalar.copy(out=dst[:, SPLIT:], in_=srcv[:, SPLIT:])
@@ -157,15 +160,18 @@ def tile_list_arousal_exemplar_scores_kernel(
         gather_tab(0)
         quant_w1(0, 0, wb, [(0, KP)])
         nc.vector.tensor_copy(
-            out=w4s[:].rearrange("p (g t m) -> p g m t", t=PACK, m=P),
-            in_=w4s_raw[:].rearrange("p (g m t) -> p g m t", t=PACK, m=P),
+            out=w4s[:].rearrange("p (g t h u) -> p g h t u", t=PACK, h=P // 16, u=16),
+            in_=w4s_raw[:].rearrange("p (g h u t) -> p g h t u", t=PACK, h=P // 16, u=16),
         )
         wb = cast_w1(1, 0, False)
         gather_tab(1)
         quant_w1(1, 0, wb, [(0, KP)])
         nc.vector.tensor_copy(
-            out=w4q[:].bitcast(U16).rearrange("p (g t m) -> p g m t", t=PACK, m=P),
-            in_=w4_raw[:].rearrange("p a n -> p (a n)").bitcast(U16).rearrange("p (g m t) -> p g m t", t=PACK, m=P),
+            out=w4q[:].bitcast(U16).rearrange("p (g t h u) -> p g h t u", t=PACK, h=P // 8, u=8),
+            in_=w4_raw[:]
+            .rearrange("p a n -> p (a n)")
+            .bitcast(U16)
+            .rearrange("p (g h u t) -> p g h t u", t=PACK, h=P // 8, u=8),
         )
         gather_tab(2)
         wb = cast_w1(2, 0, True)
@@ -189,7 +195,10 @@ def tile_list_arousal_exemplar_scores_kernel(
                     start=(a == 0),
                     stop=(a == NA - 1),
                 )
-            fs[n] = sb([P, S], F32, "f%d" % n, tag="f", bufs=NT)
+            if n == PACK:
+                fs[n] = sb([P, S], F32, "f%d" % n, tag="f_first")
+            else:
+                fs[n] = sb([P, S], F32, "f%d" % n, tag="f", bufs=NT - 1)
             nc.scalar.activation(out=fs[n][:], in_=t1[:], func=ACT.Silu, bias=b1t[:, b, i : i + 1])
 
         def stage1_y(n):
@@ -233,7 +242,7 @@ def tile_list_arousal_exemplar_scores_kernel(
 
         def slope(n):
             b, i = divmod(n, PACK)
-            sg = sb([P, NX], F32, "sg%d" % n, tag="w1q_b1")
+            sg = sb([P, NX], F32, "sg%d" % n, tag="raw_last" if n < PACK - 1 else "f_first")
             nc.scalar.activation(out=sg[:], in_=g4[b][:, i, :], func=ACT.Sign, scale=-1.0)
             nc.scalar.activation(
                 out=m4[b][:, i, :],
@@ -329,9 +338,11 @@ def tile_list_arousal_exemplar_scores_kernel(
         nc.gpsimd.tensor_tensor(out=cneg[:], in0=gxt[:], in1=wat[:], op=ALU.mult)
         for b in range(NB):
             m4[b] = sb([P, PACK, NX], F32, "m4_%d" % b, tag=("w1q_0", "w4_raw")[b])[:]
-        for n in range(NT):
+        for n in range(NT - 1):
             round_page(n)
             slope(n)
+        slope(NT - 1)
+        round_page(NT - 1)
         make_x(0)
         for c in range(NC):
             quant_page(0, c)
@@ -340,7 +351,7 @@ def tile_list_arousal_exemplar_scores_kernel(
         base_rows = base.rearrange("(t p) j -> p t j", p=P)
         baset = []
         for u in range(2):
-            baset.append(sb([P, PACK, NX], F32, "base%d" % u, tag="big", bufs=4))
+            baset.append(sb([P, PACK, NX], F32, "base%d" % u, tag="big", bufs=3))
             nc.sync.dma_start(out=baset[u][:], in_=base_rows[:, PACK * u : PACK * (u + 1), :])
         slott = sb([P, NM], F32, "slott")
         with nc.allow_non_contiguous_dma(reason="one factor for each output row"):
@@ -356,7 +367,7 @@ def tile_list_arousal_exemplar_scores_kernel(
         quant_page(1, 3)
         for mt in range(NM):
             stage2(1, mt)
-            res = sb([P, NX], F32, "res%d" % mt, tag="f", bufs=NT)
+            res = sb([P, NX], F32, "res%d" % mt, tag="f", bufs=NT - 1)
             nc.vector.scalar_tensor_tensor(
                 out=res[:],
                 in0=es[mt][:],

from contextlib import ExitStack

import concourse.mybir as mybir

K, H, T, S, T2, NX = 1536, 1024, 2048, 512, 1024, 512
FLOPS = 2 * (2 * K * H * S + H * T2 * NX)

F32 = mybir.dt.float32
BF16 = mybir.dt.bfloat16
I32 = mybir.dt.int32
U32 = mybir.dt.uint32
U16 = mybir.dt.uint16
U8 = mybir.dt.uint8
FP8X4 = mybir.dt.float8_e4m3fn_x4
FP4X4 = mybir.dt.float4_e2m1fn_x4
ALU = mybir.AluOpType
ACT = mybir.ActivationFunctionType

P = 128
PACK = 4
KP = P * PACK
NA = K // KP
NB = H // KP
NT = NB * PACK
NM = T2 // P
CH = 256
NC = T2 // CH
SPLIT = 80


def tile_list_arousal_exemplar_scores_kernel(
    tc, tab_words, tab_scales, offs, offs2, offs3, w1, b1, ga, w4_words, w4_scales, wgs, page0, wa, gx, slot, base, out
):
    nc = tc.nc
    with ExitStack() as ctx:
        keep = ctx.enter_context(tc.tile_pool(name="keep", bufs=1))
        psum = ctx.enter_context(tc.psum_pool(name="psum", bufs=1))

        def sb(shape, dtype, name, tag=None, bufs=1):
            return keep.tile(shape, dtype, name=name, tag=tag or name, bufs=bufs, align_bytes=64)

        def bank(k, name):
            return psum.tile([P, S], F32, name=name, tag="bank%d" % k)

        o1 = keep.tile([P, S // 16], U16, name="o1")
        o2 = keep.tile([P, S // 16], U16, name="o2")
        o3 = keep.tile([P, NX // 16], U16, name="o3")

        tsc = sb([P, NA * T], U8, "tsc")
        w4s_raw = sb([P, NA * H], U8, "w4s_raw")
        nc.vector.memset(tsc[:].bitcast(I32), 0)
        nc.vector.memset(w4s_raw[:].bitcast(I32), 0)

        def load_scales(eng, plane, dram):
            rows = dram.bitcast(I32).rearrange("a (q r) n -> r q a n", r=4)
            for r in range(4):
                eng.dma_start(out=plane[r:P:32, :].bitcast(I32).rearrange("q (a n) -> q a n", a=NA), in_=rows[r])

        tabw = [sb([P, T], I32, "tabw%d" % a) for a in range(NA)]
        w1raw = {}

        def load_tab(a):
            nc.sync.dma_start(out=tabw[a][:], in_=tab_words[a].rearrange("p n t -> p (n t)").bitcast(I32))

        def load_w1(a, b):
            if (a, b) == (NA - 1, NB - 1):
                w1raw[a, b] = sb([P, PACK, KP], F32, "w1raw%d%d" % (a, b), tag="raw_last")
            else:
                w1raw[a, b] = sb([P, PACK, KP], F32, "w1raw%d%d" % (a, b), tag="big", bufs=3)
            rows = w1[a * KP : (a + 1) * KP, b * KP : (b + 1) * KP]
            nc.sync.dma_start(out=w1raw[a, b][:], in_=rows.rearrange("(p j) c -> p j c", j=PACK))

        def load_vec(dram, name):
            t = sb([P, NB, PACK], F32, name)
            nc.sync.dma_start(out=t[:], in_=dram.rearrange("(b p i) -> p b i", b=NB, i=PACK))
            return t

        page = [sb([P, T2], F32, "page%d" % n) for n in range(NT)]
        page_rows = page0.rearrange("(b p i) m -> b i p m", b=NB, i=PACK)

        def load_page(n):
            nc.sync.dma_start(out=page[n][:], in_=page_rows[n // PACK, n % PACK])

        wgs_rows = wgs.rearrange("(q i) j -> q i j", i=PACK)
        wg_first = sb([P, S], F32, "wg_first")
        wg_rest = sb([P, PACK - 1, S], F32, "wg_rest")

        nc.sync.dma_start(o1[:], offs)
        load_tab(0)
        load_w1(0, 0)
        load_scales(nc.gpsimd, tsc, tab_scales)
        load_tab(1)
        load_scales(nc.gpsimd, w4s_raw, w4_scales)
        load_w1(1, 0)
        w4_raw = sb([P, NA, 2 * H], U8, "w4_raw")
        nc.sync.dma_start(out=w4_raw[:].bitcast(I32), in_=w4_words.bitcast(I32).rearrange("a p n -> p a n"))
        load_tab(2)
        load_w1(2, 0)
        b1t = load_vec(b1, "b1t")
        gat = load_vec(ga, "gat")
        nc.sync.dma_start(o2[:], offs2)
        for q in range(4):
            nc.sync.dma_start(out=wg_first[32 * q : 32 * q + 32, :], in_=wgs_rows[:, 0, :])
        load_page(0)
        nc.sync.dma_start(o3[:], offs3)
        load_page(1)
        for q in range(4):
            nc.sync.dma_start(out=wg_rest[32 * q : 32 * q + 32, :, :], in_=wgs_rows[:, 1:PACK, :])
        load_w1(0, 1)
        load_w1(1, 1)
        load_w1(2, 1)
        load_page(2)
        wat = load_vec(wa, "wat")
        gxt = load_vec(gx, "gxt")
        for n in range(3, NT):
            load_page(n)

        vq = [sb([P, S], U32, "vq%d" % a) for a in range(NA)]
        vs = [sb([P, S], U8, "vs%d" % a) for a in range(NA)]
        w1q_0 = sb([P, NA * KP], U32, "w1q_0")
        w1q_1 = sb([P, (NA - 1) * KP], U32, "w1q_1", tag="stage")
        w1q_2 = sb([P, KP], U32, "w1q_2", tag="w1q_b1")
        w1q = {(a, 0): w1q_0[:, a * KP : (a + 1) * KP] for a in range(NA)}
        w1q.update({(a, 1): w1q_1[:, a * KP : (a + 1) * KP] for a in range(NA - 1)})
        w1q[NA - 1, 1] = w1q_2[:]
        w1s = {}

        def gather_tab(a):
            nc.vector.tensor_copy(out=vq[a][:], in_=tabw[a][:].bitcast(U32).indirect(o1[:]))
            nc.vector.tensor_copy(out=vs[a][:], in_=tsc[:, a * T : (a + 1) * T].indirect(o1[:]))

        def cast_w1(a, b, split):
            if (a, b) == (NA - 1, NB - 1):
                wbf = sb([P, PACK * KP], BF16, "wbf%d%d" % (a, b), tag="hold")
            else:
                wbf = sb([P, PACK * KP], BF16, "wbf%d%d" % (a, b), tag="wbf", bufs=2)
            dst = wbf[:].rearrange("p (t m j) -> p m t j", t=PACK, j=PACK)
            srcv = w1raw[a, b][:].rearrange("p j (m t) -> p m t j", t=PACK)
            if split:
                nc.vector.tensor_copy(out=dst[:, :SPLIT], in_=srcv[:, :SPLIT])
                nc.scalar.copy(out=dst[:, SPLIT:], in_=srcv[:, SPLIT:])
            else:
                nc.scalar.copy(out=dst, in_=srcv)
            return wbf

        def quant_w1(a, b, wbf, pieces):
            w1s[a, b] = sb([P, KP], U8, "w1s%d%d" % (a, b))
            for c0, c1 in pieces:
                nc.vector.quantize_mx(
                    out=w1q[a, b][:, c0:c1].bitcast(FP8X4),
                    scales=w1s[a, b][:, c0:c1],
                    in_=wbf[:, PACK * c0 : PACK * c1],
                )

        w4q = sb([P, NA * 2 * H], U8, "w4q")
        w4s = sb([P, NA * H], U8, "w4s")
        cneg = sb([P, NB, PACK], F32, "cneg")

        wb = cast_w1(0, 0, False)
        gather_tab(0)
        quant_w1(0, 0, wb, [(0, KP)])
        nc.vector.tensor_copy(
            out=w4s[:].rearrange("p (g t h u) -> p g h t u", t=PACK, h=P // 16, u=16),
            in_=w4s_raw[:].rearrange("p (g h u t) -> p g h t u", t=PACK, h=P // 16, u=16),
        )
        wb = cast_w1(1, 0, False)
        gather_tab(1)
        quant_w1(1, 0, wb, [(0, KP)])
        nc.vector.tensor_copy(
            out=w4q[:].bitcast(U16).rearrange("p (g t h u) -> p g h t u", t=PACK, h=P // 8, u=8),
            in_=w4_raw[:]
            .rearrange("p a n -> p (a n)")
            .bitcast(U16)
            .rearrange("p (g h u t) -> p g h t u", t=PACK, h=P // 8, u=8),
        )
        gather_tab(2)
        wb = cast_w1(2, 0, True)
        quant_w1(2, 0, wb, [(0, P), (P, 2 * P), (2 * P, KP)])

        fs = {}
        ys = {}
        hs = {}

        def stage1_t(n):
            b, i = divmod(n, PACK)
            t1 = bank(n % 2 if b == 0 else n, "t1_%d" % n)
            cols = slice(i * P, (i + 1) * P)
            for a in range(NA):
                nc.tensor.matmul_mx(
                    out=t1[:],
                    lhsT=w1q[a, b][:, cols].bitcast(FP8X4),
                    lhsT_scale=w1s[a, b][:, cols],
                    rhs=vq[a][:].bitcast(FP8X4),
                    rhs_scale=vs[a][:],
                    start=(a == 0),
                    stop=(a == NA - 1),
                )
            if n == PACK:
                fs[n] = sb([P, S], F32, "f%d" % n, tag="f_first")
            else:
                fs[n] = sb([P, S], F32, "f%d" % n, tag="f", bufs=NT - 1)
            nc.scalar.activation(out=fs[n][:], in_=t1[:], func=ACT.Silu, bias=b1t[:, b, i : i + 1])

        def stage1_y(n):
            b, i = divmod(n, PACK)
            y4 = bank(2 + n % 2, "y4_%d" % n)
            for a in range(NA):
                c0 = a * H + b * KP + i * P
                nc.tensor.matmul_mx(
                    out=y4[:],
                    lhsT=w4q[:, 2 * c0 : 2 * (c0 + P)].bitcast(FP4X4),
                    lhsT_scale=w4s[:, c0 : c0 + P],
                    rhs=vq[a][:].bitcast(FP8X4),
                    rhs_scale=vs[a][:],
                    start=(a == 0),
                    stop=(a == NA - 1),
                )
            ys[n] = y4

        def combine(n):
            b, i = divmod(n, PACK)
            if n == PACK - 2:
                hs[n] = sb([P, S], F32, "h%d" % n, tag="hold")
            else:
                hs[n] = sb([P, S], F32, "h%d" % n, tag="h", bufs=3)
            nc.vector.scalar_tensor_tensor(
                out=hs[n][:], in0=fs[n][:], scalar=gat[:, b, i : i + 1], in1=ys[n][:], op0=ALU.mult, op1=ALU.add
            )

        def scatter(n):
            i = n % PACK
            wg = wg_first[:] if i == 0 else wg_rest[:, i - 1, :]
            nc.vector.tensor_tensor(out=page[n][:].indirect(o2[:]), in0=hs[n][:], in1=wg, op=ALU.mult)

        g4 = [sb([P, PACK, NX], F32, "g4_%d" % b) for b in range(NB)]
        m4 = {}
        stage = {}

        def pick(n):
            b, i = divmod(n, PACK)
            nc.vector.tensor_copy(out=g4[b][:, i, :], in_=page[n][:].indirect(o3[:]))

        def slope(n):
            b, i = divmod(n, PACK)
            sg = sb([P, NX], F32, "sg%d" % n, tag="raw_last" if n < PACK - 1 else "f_first")
            nc.scalar.activation(out=sg[:], in_=g4[b][:, i, :], func=ACT.Sign, scale=-1.0)
            nc.scalar.activation(
                out=m4[b][:, i, :],
                in_=sg[:],
                func=ACT.Identity,
                scale=cneg[:, b, i : i + 1],
                bias=gxt[:, b, i : i + 1],
            )

        pbf = {}
        pq = {}
        ps = {}

        def round_page(n):
            b, i = divmod(n, PACK)
            if i == 0:
                stage[b] = sb([P, PACK - 1, T2], BF16, "stage%d" % b, tag="stage")[:]
            if i < PACK - 1:
                nc.scalar.copy(out=stage[b][:, i, :], in_=page[n][:])
            if i == PACK - 2:
                for c in range(NC):
                    pbf[b, c] = sb([P, CH * PACK], BF16, "pbf%d%d" % (b, c), tag="pbf%d%d" % (b, c))
                    nc.scalar.copy(
                        out=pbf[b, c][:].rearrange("p (c u t) -> p c t u", u=4, t=PACK)[:, :, : PACK - 1, :],
                        in_=stage[b][:, :, c * CH : (c + 1) * CH].rearrange("p t (c u) -> p c t u", u=4),
                    )
            if i == PACK - 1:
                for c in range(NC):
                    nc.scalar.copy(
                        out=pbf[b, c][:].rearrange("p (c t) -> p c t", t=PACK)[:, :, PACK - 1],
                        in_=page[n][:, c * CH : (c + 1) * CH],
                    )

        def quant_page(b, c):
            pq[b, c] = sb([P, CH], U32, "pq%d%d" % (b, c))
            ps[b, c] = sb([P, CH], U8, "ps%d%d" % (b, c))
            nc.vector.quantize_mx(out=pq[b, c][:].bitcast(FP8X4), scales=ps[b, c][:], in_=pbf[b, c][:])

        xbf = {}
        xq = {}
        xs = {}

        def make_x(b):
            xbf[b] = sb([P, NX * PACK], BF16, "xbf%d" % b, tag="wbf", bufs=2)
            nc.vector.tensor_tensor(
                out=xbf[b][:].rearrange("p (c u t) -> p c t u", u=4, t=PACK),
                in0=g4[b][:].rearrange("p t (c u) -> p c t u", u=4),
                in1=m4[b].rearrange("p t (c u) -> p c t u", u=4),
                op=ALU.mult,
            )

        def quant_x(b):
            xq[b] = sb([P, NX], U32, "xq%d" % b)
            xs[b] = sb([P, NX], U8, "xs%d" % b)
            nc.vector.quantize_mx(out=xq[b][:].bitcast(FP8X4), scales=xs[b][:], in_=xbf[b][:])

        es = {}

        def stage2(b, mt):
            if b == 0:
                es[mt] = bank(mt, "e%d" % mt)
            c, r = divmod(mt * P, CH)
            nc.tensor.matmul_mx(
                out=es[mt][:],
                lhsT=pq[b, c][:, r : r + P].bitcast(FP8X4),
                lhsT_scale=ps[b, c][:, r : r + P],
                rhs=xq[b][:].bitcast(FP8X4),
                rhs_scale=xs[b][:],
                start=(b == 0),
                stop=(b == NB - 1),
            )

        for n in range(PACK):
            stage1_t(n)
            if n < 2:
                stage1_y(n)
        combine(0)
        stage1_y(2)
        for n in range(NT):
            scatter(n)
            if n == 0:
                for a in range(NA):
                    quant_w1(a, 1, cast_w1(a, 1, False), [(0, KP)])
            if n == 1:
                for n1 in range(PACK, NT):
                    stage1_t(n1)
            if n + 1 < NT:
                combine(n + 1)
            if n + 3 < NT:
                stage1_y(n + 3)
            pick(n)

        nc.gpsimd.tensor_tensor(out=cneg[:], in0=gxt[:], in1=wat[:], op=ALU.mult)
        for b in range(NB):
            m4[b] = sb([P, PACK, NX], F32, "m4_%d" % b, tag=("w1q_0", "w4_raw")[b])[:]
        for n in range(NT - 1):
            round_page(n)
            slope(n)
        slope(NT - 1)
        round_page(NT - 1)
        make_x(0)
        for c in range(NC):
            quant_page(0, c)
        quant_x(0)

        base_rows = base.rearrange("(t p) j -> p t j", p=P)
        baset = []
        for u in range(2):
            baset.append(sb([P, PACK, NX], F32, "base%d" % u, tag="big", bufs=3))
            nc.sync.dma_start(out=baset[u][:], in_=base_rows[:, PACK * u : PACK * (u + 1), :])
        slott = sb([P, NM], F32, "slott")
        with nc.allow_non_contiguous_dma(reason="one factor for each output row"):
            nc.sync.dma_start(out=slott[:], in_=slot.rearrange("(t p) -> p t", p=P))

        for mt in (4, 5, 6, 7, 0, 1, 2, 3):
            stage2(0, mt)
        quant_page(1, 0)
        make_x(1)
        quant_page(1, 1)
        quant_x(1)
        quant_page(1, 2)
        quant_page(1, 3)
        for mt in range(NM):
            stage2(1, mt)
            res = sb([P, NX], F32, "res%d" % mt, tag="f", bufs=NT - 1)
            nc.vector.scalar_tensor_tensor(
                out=res[:],
                in0=es[mt][:],
                scalar=slott[:, mt : mt + 1],
                in1=baset[mt // PACK][:, mt % PACK, :],
                op0=ALU.mult,
                op1=ALU.add,
            )
            nc.sync.dma_start(out=out[mt * P : (mt + 1) * P, :], in_=res[:])
